import numpy as np, ml_dtypes
CORES = [100,101,102,103,108,109,110,111]
N = 8
import mx_ref
NC, G = 384, 4
M = NC // N
C = np.float32(0.031)
BF = ml_dtypes.bfloat16
def cut(t, i, w=512):
    return t[:, w * i:w * i + w]
def tile(rs):
    return np.stack(rs, axis=2).reshape(128, -1).astype(BF)
def layer(w, X):
    out = []
    for i in range(G):
        for t in range(len(X)):
            p = mx_ref.matmul(mx_ref.quantize(cut(w, len(X) * i + t)), X[t])
            z = p if t == 0 else z + p
        out.append(z)
    return out
def act(Z):
    return [np.maximum(z, 0) * C for z in Z]
def setup_inputs(rng):
    def f(*shape):
        return mx_ref.flush((rng.standard_normal(shape, dtype=np.float32) * np.exp2(rng.integers(-2, 3, shape[:-1] + (1,)))).astype(BF))
    return {"x": f(N, 128, 4 * NC), "w1": f(N, 128, G * 512), "w2": f(N, 128, 512)}
def setup_inputs_blocks(rng):
    d = setup_inputs(rng)
    for k in ("x", "w1", "w2"): d[k] = mx_ref.spread(d[k], rng, 4)
    return d
def setup_inputs_wide(rng):
    d = setup_inputs(rng)
    for k in ("x", "w1", "w2"): d[k] = mx_ref.flush((d[k].astype(np.float32) * np.exp2(rng.integers(-8, 9, (N, 1, 1))).astype(np.float32)).astype(BF))
    return d
def setup_inputs_zeros(rng):
    d = setup_inputs(rng); v = d["x"].reshape(N, 128, -1, 4).copy()
    v[np.broadcast_to((rng.random((N, 1, v.shape[2], 1)) < 0.33), v.shape)] = 0
    d["x"] = v.reshape(d["x"].shape)
    return d
def reference(x, w1, w2):
    h = [tile(act(layer(w1[j], [mx_ref.quantize(x[j])]))) for j in range(N)]
    y = np.zeros((N, 128, NC), np.float32)
    for r in range(N):
        t = np.concatenate([cut(h[j], r, 4 * M) for j in range(N)], axis=1)
        y[r] = mx_ref.matmul(mx_ref.quantize(w2[r]), mx_ref.quantize(t))
    return {"y": y}

@@ -1,0 +1,270 @@
+from concourse.bass import DstId, RemoteDMATransfer
+from concourse.mybir import dt, AluOpType, ActivationFunctionType
+
+N = 8
+NC = 384
+RUN = NC // N
+HALF = NC // 2
+SIDE = HALF - RUN
+L = HALF // RUN
+CONST = 0.031
+BANK = 512
+
+AIDS = True
+FAR_SEQ = "aid"
+NEAR_HIGH = False
+NEAR_TURN = True
+W1_PARTS = 2
+
+CODE, PLANE, BF = "float8_e4m3fn_x4", "uint8", "bfloat16"
+SCRATCH = {
+    "xf": ("sbuf", [128, 4 * HALF], BF), "xn": ("sbuf", [128, 4 * HALF], BF),
+    "w1s": ("sbuf", [128, 4 * 512], BF), "w2s": ("sbuf", [128, 512], BF),
+    "xfq": ("sbuf", [128, HALF], CODE), "xfp": ("sbuf", [128, HALF], PLANE),
+    "xnq": ("sbuf", [128, HALF], CODE), "xnp": ("sbuf", [128, HALF], PLANE),
+    "w1q": ("sbuf", [128, 512], CODE), "w1p": ("sbuf", [128, 512], PLANE),
+    "w2q": ("sbuf", [128, 128], CODE), "w2p": ("sbuf", [128, 128], PLANE),
+    "hf": ("sbuf", [128, 4 * HALF], BF), "hn": ("sbuf", [128, 4 * HALF], BF),
+    "fq": ("sbuf", [128, SIDE + HALF + SIDE], CODE), "fp": ("sbuf", [128, SIDE + HALF + SIDE], PLANE),
+    "nq": ("sbuf", [128, HALF], CODE), "npl": ("sbuf", [128, HALF], PLANE),
+    "gq": ("sbuf", [128, HALF], CODE), "gp": ("sbuf", [128, HALF], PLANE),
+    "lnq": ("sbuf", [128, SIDE], CODE), "lnp": ("sbuf", [128, SIDE], PLANE),
+    "lfq": ("sbuf", [128, HALF], CODE), "lfp": ("sbuf", [128, HALF], PLANE),
+    "ys": ("sbuf", [128, NC], "float32"),
+    "ps": ("psum", [128, 8 * BANK], "float32"),
+}
+SEMAPHORES = (["ld_xf", "ld_xn", "ld_v", "q_xf", "q_xn", "q_v", "q_hf", "q_hn", "a_f", "a_n", "m_own", "m_near", "m_far",
+               "e_near", "e_far", "st", "near_arr", "far_arr", "gat_q", "gat_p", "sent"]
+              + ["ld_w%d" % i for i in range(4)] + ["q_w%d" % i for i in range(4)]
+              + ["m_f%d" % i for i in range(4)] + ["m_n%d" % i for i in range(4)])
+
+
+def _bits(m):
+    return [e for e in range(m.bit_length()) if (m >> e) & 1]
+
+
+def _plan(T, topo):
+    cores = list(T.cores)
+    plan = {}
+    for ch in sorted({topo.chip(c) for c in cores}):
+        mem = [c for c in cores if topo.chip(c) == ch]
+        far = [c for c in cores if topo.chip(c) != ch]
+        ports = [c for c in range(topo.CORES_PER_CHIP * topo.CHIPS)
+                 if topo.chip(c) == ch and all(topo.may_write(c, d) for d in far)]
+        own = [c for c in ports if c in mem]
+        aid = [c for c in ports if c not in mem]
+        ford = {c: list(range(L)) for c in mem}
+        if AIDS:
+            gate = [(own[-1], "front"), (aid[0], "aid"), (aid[1], "aid"), (own[0], "back")]
+        else:
+            gate = [(own[-1], "front"), (own[0], "back"), (own[0], "front"), (own[-1], "back")]
+            ford[own[0]] = [2, 3, 0, 1]
+        plan[ch] = {"mem": mem, "far": far, "gate": gate, "ford": ford}
+    return plan
+
+
+def _slot(P, i):
+    G, kind = P["gate"][i]
+    if kind == "aid":
+        return list(range(L)), 0, "gq", "gp"
+    gl = P["mem"].index(G)
+    if kind == "front":
+        return [(gl + 1 + k) % L for k in range(L)], 0, "fq", "fp"
+    return [(gl + k) % L for k in range(L)], SIDE + HALF - RUN, "fq", "fp"
+
+
+def _deal(n, es, turn):
+    if n == 3:
+        k = len(es) // 4
+        return [es[2 * k:3 * k], es[3 * k:], es[:2 * k]] if turn else [es[:k], es[k:2 * k], es[2 * k:]]
+    k = len(es) // n
+    return [es[k * i:k * i + k] for i in range(n)]
+
+
+def _calls(P, topo, src):
+    mem = P["mem"]
+    todo = [i for i in range(L) if P["gate"][i][0] != src]
+    aid = [i for i in todo if P["gate"][i][1] == "aid"]
+    own = [i for i in todo if P["gate"][i][1] != "aid"]
+    seq = {"together": ((todo, "q"), (todo, "p")), "together_p": ((todo, "p"), (todo, "q")),
+           "aid": ((aid, "q"), (aid, "p"), (own, "q"), (own, "p")),
+           "aid_qq": ((aid, "q"), (own, "q"), (aid, "p"), (own, "p")),
+           "aid_p": ((aid, "p"), (aid, "q"), (own, "q"), (own, "p"))}[FAR_SEQ]
+    out = []
+    for grp, kind in seq:
+        if grp:
+            es = _bits(topo.mask(src, P["gate"][grp[0]][0]))
+            out.append([(P["gate"][i][0], "far", kind, i, e) for i, e in zip(grp, _deal(len(grp), es, kind == "p"))])
+    near = [j for j in range(L) if mem[j] != src]
+    es = _bits(topo.mask(src, mem[near[0]]))
+    if NEAR_HIGH and len(todo) < L:
+        off = _bits(topo.mask(src, P["far"][0]))
+        es = [e for e in es if e not in off]
+    for kind in ("q", "p"):
+        out.append([(mem[j], "near", kind, j, e) for j, e in zip(near, _deal(len(near), es, kind == "p" and NEAR_TURN))])
+    return out
+
+
+def _due(P, topo, dst, tag, kinds):
+    return sum(len(it[4]) for s in P["mem"] for call in _calls(P, topo, s) for it in call
+               if it[0] == dst and it[1] == tag and it[2] in kinds)
+
+
+def _cross(P, topo, G):
+    serves = [i for i in range(L) if P["gate"][i][0] == G]
+    return list(zip(serves, _deal(len(serves), _bits(topo.mask(G, P["far"][serves[0]])), False)))
+
+
+def _pieces(blocks):
+    out, p = [], 0
+    while p < len(blocks):
+        e = p + 1
+        while e < len(blocks) and blocks[e] == blocks[e - 1] + 1:
+            e += 1
+        out.append((p, e, blocks[p]))
+        p = e
+    return out
+
+
+def _fan(g, topo, items, local_sem):
+    trs = []
+    for d, dst, src, sem, es in items:
+        rid, pid, _ = topo.addr(d)
+        trs.append(RemoteDMATransfer(dst_ids=[DstId(rid=rid, pnc=pid)], dma_engine_mask=sum(1 << e for e in es),
+                                     remote_sem=sem, src=src, dst=dst))
+    g.remote_dma_fused(trs, local_sem=local_sem)
+    return sum(len(it[4]) for it in items)
+
+
+def rank_program(g, core, T, topo):
+    S = T.sem
+    plan = _plan(T, topo)
+    if topo.chip(core) not in plan:
+        return
+    P = plan[topo.chip(core)]
+    mem, far = P["mem"], P["far"]
+    rank = T.rank_of(core)
+    gate = core in [G for G, _ in P["gate"]]
+    if rank is None and not gate:
+        return
+    u8 = dt.uint8
+    sent = 0
+
+    if rank is not None:
+        sy, sc, v, pe = g.sync, g.scalar, g.vector, g.tensor
+        Q = plan[topo.chip(far[0])]
+        q = mem.index(core)
+        ford = P["ford"][core]
+        ps = T.ps
+
+        fl = _pieces(ford)
+        for n, (p, e, i) in enumerate(fl):
+            c0 = 4 * RUN * T.rank_of(far[i])
+            (sy if n == 0 else sc).dma_start(T.xf[:, 4 * RUN * p:4 * RUN * e], T.x[:, c0:c0 + 4 * RUN * (e - p)]).then_inc(S.ld_xf, 16)
+        wid = 4 * 512 // W1_PARTS
+        for n in range(W1_PARTS):
+            (sc if n == 0 else sy).dma_start(T.w1s[:, wid * n:wid * (n + 1)], T.w1[:, wid * n:wid * (n + 1)]).then_inc(S["ld_w%d" % n], 16)
+        c0 = 4 * RUN * T.rank_of(mem[0])
+        sy.dma_start(T.xn[:], T.x[:, c0:c0 + 4 * HALF]).then_inc(S.ld_xn, 16)
+        sy.dma_start(T.w2s[:], T.w2[:]).then_inc(S.ld_v, 16)
+
+        for half, (xq, xp, sx, tag) in enumerate(((T.xfq, T.xfp, S.q_xf, "m_f%d"), (T.xnq, T.xnp, S.q_xn, "m_n%d"))):
+            pe.wait_ge(sx, 1)
+            for b in range(4):
+                if half == 0:
+                    pe.wait_ge(S["q_w%d" % b], 1)
+                k = 4 * half + b
+                pe.matmul_mx(ps[:, BANK * k:BANK * k + HALF], T.w1q[:, 128 * b:128 * b + 128], T.w1p[:, 128 * b:128 * b + 128],
+                             xq[:], xp[:], True, True).then_inc(S[tag % b], 1)
+        win = 0 if RUN * q + RUN <= 128 else HALF - 128
+        pe.wait_ge(S.a_f, 4)
+        pe.wait_ge(S.q_hn, 1)
+        pe.wait_ge(S.q_v, 1)
+        pe.matmul_mx(ps[:, 0:128], T.w2q[:], T.w2p[:], T.nq[:, win:win + 128], T.npl[:, win:win + 128], True, True).then_inc(S.m_own, 1)
+        pe.wait_ge(S.near_arr, _due(P, topo, core, "near", "qp"))
+        pe.matmul_mx(ps[:, BANK:BANK + SIDE], T.w2q[:], T.w2p[:], T.lnq[:], T.lnp[:], True, True).then_inc(S.m_near, 1)
+        pe.wait_ge(S.far_arr, 2 * sum(len(es) for i, es in _cross(Q, topo, Q["gate"][q][0]) if i == q))
+        pe.matmul_mx(ps[:, 2 * BANK:2 * BANK + HALF], T.w2q[:], T.w2p[:], T.lfq[:], T.lfp[:], True, True).then_inc(S.m_far, 1)
+
+        def act_s(h, k, b, sm, sa):
+            sc.wait_ge(sm, 1)
+            sc.activation(h[:, b:4 * HALF:4], ps[:, BANK * k:BANK * k + HALF], ActivationFunctionType.Relu, scale=CONST).then_inc(sa, 1)
+
+        def act_v(h, k, b, sm, sa):
+            v.wait_ge(sm, 1)
+            v.tensor_scalar(h[:, b:4 * HALF:4], ps[:, BANK * k:BANK * k + HALF], 0.0, CONST, AluOpType.max, AluOpType.mult).then_inc(sa, 1)
+
+        for b in (0, 1, 2):
+            act_s(T.hf, b, b, S["m_f%d" % b], S.a_f)
+        for b in (0, 2):
+            act_s(T.hn, 4 + b, b, S["m_n%d" % b], S.a_n)
+        sc.wait_ge(S.m_own, 1)
+        o = RUN * q - win
+        sc.activation(T.ys[:, RUN * rank:RUN * rank + RUN], ps[:, o:o + RUN], ActivationFunctionType.Copy).then_inc(S.e_near, 1)
+        sc.wait_ge(S.m_near, 1)
+        near_pc = _pieces([T.rank_of(mem[j]) for j in range(L) if j != q])
+        for p, e, blk in near_pc:
+            sc.activation(T.ys[:, RUN * blk:RUN * (blk + e - p)], ps[:, BANK + RUN * p:BANK + RUN * e], ActivationFunctionType.Copy).then_inc(S.e_near, 1)
+
+        v.wait_ge(S.ld_xf, 16 * len(fl))
+        v.quantize_mx(T.xfq[:], T.xfp[:], T.xf[:]).then_inc(S.q_xf, 1)
+        for b in range(4):
+            if b % (4 // W1_PARTS) == 0:
+                v.wait_ge(S["ld_w%d" % (b // (4 // W1_PARTS))], 16)
+            v.quantize_mx(T.w1q[:, 128 * b:128 * b + 128], T.w1p[:, 128 * b:128 * b + 128], T.w1s[:, 512 * b:512 * b + 512]).then_inc(S["q_w%d" % b], 1)
+        act_v(T.hf, 3, 3, S.m_f3, S.a_f)
+        v.wait_ge(S.a_f, 4)
+        v.quantize_mx(T.fq[:, SIDE:SIDE + HALF], T.fp[:, SIDE:SIDE + HALF], T.hf[:]).then_inc(S.q_hf, 1)
+        v.wait_ge(S.ld_xn, 16)
+        v.quantize_mx(T.xnq[:], T.xnp[:], T.xn[:]).then_inc(S.q_xn, 1)
+        act_v(T.hn, 5, 1, S.m_n1, S.a_n)
+        act_v(T.hn, 7, 3, S.m_n3, S.a_n)
+        v.wait_ge(S.a_n, 4)
+        v.quantize_mx(T.nq[:], T.npl[:], T.hn[:]).then_inc(S.q_hn, 1)
+        v.wait_ge(S.ld_v, 16)
+        v.quantize_mx(T.w2q[:], T.w2p[:], T.w2s[:]).then_inc(S.q_v, 1)
+        v.wait_ge(S.m_far, 1)
+        far_pc = _pieces([T.rank_of(far[j]) for j in _slot(Q, q)[0]])
+        for p, e, blk in far_pc:
+            v.tensor_copy(T.ys[:, RUN * blk:RUN * (blk + e - p)], ps[:, 2 * BANK + RUN * p:2 * BANK + RUN * e]).then_inc(S.e_far, 1)
+
+        c0, c1 = RUN * T.rank_of(mem[0]), RUN * T.rank_of(far[0])
+        sy.wait_ge(S.e_near, 1 + len(near_pc))
+        sy.dma_start(T.y[:, c0:c0 + HALF], T.ys[:, c0:c0 + HALF]).then_inc(S.st, 16)
+        sy.wait_ge(S.e_far, len(far_pc))
+        sy.dma_start(T.y[:, c1:c1 + HALF], T.ys[:, c1:c1 + HALF]).then_inc(S.st, 16)
+        sy.wait_ge(S.st, 32)
+
+        seen = []
+        for call in _calls(P, topo, core):
+            if call[0][1] not in seen:
+                seen.append(call[0][1])
+                g.wait_ge(S.q_hf if call[0][1] == "far" else S.q_hn, 1)
+            items = []
+            for d, tag, kind, i, es in call:
+                if tag == "far":
+                    order, base, bq, bp = _slot(P, i)
+                    a, c, sq, sp = SIDE + RUN * ford.index(i), base + RUN * order.index(q), T.fq, T.fp
+                    sem = S.gat_q if kind == "q" else S.gat_p
+                else:
+                    a, c, bq, bp, sq, sp, sem = RUN * i, RUN * (q if q < i else q - 1), "lnq", "lnp", T.nq, T.npl, S.near_arr
+                if kind == "q":
+                    items.append((d, T[bq][:, c:c + RUN].bitcast(u8), sq[:, a:a + RUN].bitcast(u8), sem, es))
+                else:
+                    items.append((d, T[bp][:, c:c + RUN], sp[:, a:a + RUN], sem, es))
+            sent += _fan(g, topo, items, S.sent)
+
+    if gate:
+        other = [s for s in mem if s != core][0]
+        kinds = [call[0][2] for call in _calls(P, topo, other) if call[0][1] == "far" and core in [it[0] for it in call]]
+        for kind in kinds:
+            g.wait_ge(S.gat_q if kind == "q" else S.gat_p, _due(P, topo, core, "far", kind))
+            items = []
+            for i, es in _cross(P, topo, core):
+                _, base, bq, bp = _slot(P, i)
+                if kind == "q":
+                    items.append((far[i], T.lfq[:].bitcast(u8), T[bq][:, base:base + HALF].bitcast(u8), S.far_arr, es))
+                else:
+                    items.append((far[i], T.lfp[:], T[bp][:, base:base + HALF], S.far_arr, es))
+            sent += _fan(g, topo, items, S.sent)
+    g.wait_ge(S.sent, sent)

@@ -9,12 +9,7 @@ SIDE = HALF - RUN
 L = HALF // RUN
 CONST = 0.031
 BANK = 512
-
-AIDS = True
-FAR_SEQ = "aid"
-NEAR_HIGH = False
-NEAR_TURN = True
-W1_PARTS = 2
+W1_PARTS = 4
 
 CODE, PLANE, BF = "float8_e4m3fn_x4", "uint8", "bfloat16"
 SCRATCH = {
@@ -34,7 +29,7 @@ SCRATCH = {
     "ps": ("psum", [128, 8 * BANK], "float32"),
 }
 SEMAPHORES = (["ld_xf", "ld_xn", "ld_v", "q_xf", "q_xn", "q_v", "q_hf", "q_hn", "a_f", "a_n", "m_own", "m_near", "m_far",
-               "e_near", "e_far", "st", "near_arr", "far_arr", "gat_q", "gat_p", "sent"]
+               "e_near", "e_f0", "e_f1", "st", "st_b", "near_arr", "far_arr", "gat_q", "gat_p", "sent"]
               + ["ld_w%d" % i for i in range(4)] + ["q_w%d" % i for i in range(4)]
               + ["m_f%d" % i for i in range(4)] + ["m_n%d" % i for i in range(4)])
 
@@ -53,24 +48,29 @@ def _plan(T, topo):
                  if topo.chip(c) == ch and all(topo.may_write(c, d) for d in far)]
         own = [c for c in ports if c in mem]
         aid = [c for c in ports if c not in mem]
-        ford = {c: list(range(L)) for c in mem}
-        if AIDS:
-            gate = [(own[-1], "front"), (aid[0], "aid"), (aid[1], "aid"), (own[0], "back")]
-        else:
-            gate = [(own[-1], "front"), (own[0], "back"), (own[0], "front"), (own[-1], "back")]
-            ford[own[0]] = [2, 3, 0, 1]
-        plan[ch] = {"mem": mem, "far": far, "gate": gate, "ford": ford}
+        gate = [(own[-1], "front"), (aid[0], "aid"), (aid[1], "aid"), (own[0], "back")]
+        plan[ch] = {"mem": mem, "far": far, "gate": gate, "own": own}
     return plan
 
 
 def _slot(P, i):
     G, kind = P["gate"][i]
+    mem = P["mem"]
+    plain = [j for j in range(L) if mem[j] not in P["own"]]
+    port = [j for j in range(L) if mem[j] in P["own"]]
     if kind == "aid":
-        return list(range(L)), 0, "gq", "gp"
-    gl = P["mem"].index(G)
+        return plain + port, 0, "gq", "gp"
+    gl = mem.index(G)
+    rest = [j for j in port if j != gl]
     if kind == "front":
-        return [(gl + 1 + k) % L for k in range(L)], 0, "fq", "fp"
-    return [(gl + k) % L for k in range(L)], SIDE + HALF - RUN, "fq", "fp"
+        return rest + plain + [gl], 0, "fq", "fp"
+    return [gl] + plain + rest, SIDE + HALF - RUN, "fq", "fp"
+
+
+def _held(P, i):
+    G = P["gate"][i][0]
+    have = [k for k, j in enumerate(_slot(P, i)[0]) if P["mem"][j] not in P["own"] or P["mem"][j] == G]
+    return have[0], have[-1] + 1
 
 
 def _deal(n, es, turn):
@@ -83,25 +83,23 @@ def _deal(n, es, turn):
 
 def _calls(P, topo, src):
     mem = P["mem"]
-    todo = [i for i in range(L) if P["gate"][i][0] != src]
-    aid = [i for i in todo if P["gate"][i][1] == "aid"]
-    own = [i for i in todo if P["gate"][i][1] != "aid"]
-    seq = {"together": ((todo, "q"), (todo, "p")), "together_p": ((todo, "p"), (todo, "q")),
-           "aid": ((aid, "q"), (aid, "p"), (own, "q"), (own, "p")),
-           "aid_qq": ((aid, "q"), (own, "q"), (aid, "p"), (own, "p")),
-           "aid_p": ((aid, "p"), (aid, "q"), (own, "q"), (own, "p"))}[FAR_SEQ]
-    out = []
-    for grp, kind in seq:
-        if grp:
-            es = _bits(topo.mask(src, P["gate"][grp[0]][0]))
-            out.append([(P["gate"][i][0], "far", kind, i, e) for i, e in zip(grp, _deal(len(grp), es, kind == "p"))])
     near = [j for j in range(L) if mem[j] != src]
-    es = _bits(topo.mask(src, mem[near[0]]))
-    if NEAR_HIGH and len(todo) < L:
+    on = _bits(topo.mask(src, mem[near[0]]))
+    todo = [i for i in range(L) if P["gate"][i][0] != src]
+    out = []
+    if src in P["own"]:
         off = _bits(topo.mask(src, P["far"][0]))
-        es = [e for e in es if e not in off]
+        high = [e for e in on if e not in off]
+        out.append([(P["far"][i], "dir", "q", i, e) for i, e in zip(todo, _deal(len(todo), off, False))])
+        out.append([(P["gate"][i][0], "far", "p", i, e) for i, e in zip(todo, _deal(len(todo), high, False))])
+    else:
+        aid = [i for i in todo if P["gate"][i][1] == "aid"]
+        own = [i for i in todo if P["gate"][i][1] != "aid"]
+        h = len(on) // 2
+        for grp, kind, es in ((aid, "q", on[:h]), (own, "q", on[h:]), (aid + own, "p", on)):
+            out.append([(P["gate"][i][0], "far", kind, i, e) for i, e in zip(grp, _deal(len(grp), es, kind == "p"))])
     for kind in ("q", "p"):
-        out.append([(mem[j], "near", kind, j, e) for j, e in zip(near, _deal(len(near), es, kind == "p" and NEAR_TURN))])
+        out.append([(mem[j], "near", kind, j, e) for j, e in zip(near, _deal(len(near), on, kind == "p"))])
     return out
 
 
@@ -154,18 +152,15 @@ def rank_program(g, core, T, topo):
         sy, sc, v, pe = g.sync, g.scalar, g.vector, g.tensor
         Q = plan[topo.chip(far[0])]
         q = mem.index(core)
-        ford = P["ford"][core]
         ps = T.ps
 
-        fl = _pieces(ford)
-        for n, (p, e, i) in enumerate(fl):
-            c0 = 4 * RUN * T.rank_of(far[i])
-            (sy if n == 0 else sc).dma_start(T.xf[:, 4 * RUN * p:4 * RUN * e], T.x[:, c0:c0 + 4 * RUN * (e - p)]).then_inc(S.ld_xf, 16)
+        c0 = 4 * RUN * T.rank_of(far[0])
+        sy.dma_start(T.xf[:], T.x[:, c0:c0 + 4 * HALF]).then_inc(S.ld_xf, 16)
         wid = 4 * 512 // W1_PARTS
         for n in range(W1_PARTS):
-            (sc if n == 0 else sy).dma_start(T.w1s[:, wid * n:wid * (n + 1)], T.w1[:, wid * n:wid * (n + 1)]).then_inc(S["ld_w%d" % n], 16)
+            (sc if n % 2 == 0 else sy).dma_start(T.w1s[:, wid * n:wid * (n + 1)], T.w1[:, wid * n:wid * (n + 1)]).then_inc(S["ld_w%d" % n], 16)
         c0 = 4 * RUN * T.rank_of(mem[0])
-        sy.dma_start(T.xn[:], T.x[:, c0:c0 + 4 * HALF]).then_inc(S.ld_xn, 16)
+        sc.dma_start(T.xn[:], T.x[:, c0:c0 + 4 * HALF]).then_inc(S.ld_xn, 16)
         sy.dma_start(T.w2s[:], T.w2[:]).then_inc(S.ld_v, 16)
 
         for half, (xq, xp, sx, tag) in enumerate(((T.xfq, T.xfp, S.q_xf, "m_f%d"), (T.xnq, T.xnp, S.q_xn, "m_n%d"))):
@@ -183,7 +178,7 @@ def rank_program(g, core, T, topo):
         pe.matmul_mx(ps[:, 0:128], T.w2q[:], T.w2p[:], T.nq[:, win:win + 128], T.npl[:, win:win + 128], True, True).then_inc(S.m_own, 1)
         pe.wait_ge(S.near_arr, _due(P, topo, core, "near", "qp"))
         pe.matmul_mx(ps[:, BANK:BANK + SIDE], T.w2q[:], T.w2p[:], T.lnq[:], T.lnp[:], True, True).then_inc(S.m_near, 1)
-        pe.wait_ge(S.far_arr, 2 * sum(len(es) for i, es in _cross(Q, topo, Q["gate"][q][0]) if i == q))
+        pe.wait_ge(S.far_arr, 2 * sum(len(es) for i, es in _cross(Q, topo, Q["gate"][q][0]) if i == q) + _due(Q, topo, core, "dir", "q"))
         pe.matmul_mx(ps[:, 2 * BANK:2 * BANK + HALF], T.w2q[:], T.w2p[:], T.lfq[:], T.lfp[:], True, True).then_inc(S.m_far, 1)
 
         def act_s(h, k, b, sm, sa):
@@ -206,17 +201,17 @@ def rank_program(g, core, T, topo):
         for p, e, blk in near_pc:
             sc.activation(T.ys[:, RUN * blk:RUN * (blk + e - p)], ps[:, BANK + RUN * p:BANK + RUN * e], ActivationFunctionType.Copy).then_inc(S.e_near, 1)
 
-        v.wait_ge(S.ld_xf, 16 * len(fl))
+        v.wait_ge(S.ld_xf, 16)
         v.quantize_mx(T.xfq[:], T.xfp[:], T.xf[:]).then_inc(S.q_xf, 1)
         for b in range(4):
             if b % (4 // W1_PARTS) == 0:
                 v.wait_ge(S["ld_w%d" % (b // (4 // W1_PARTS))], 16)
             v.quantize_mx(T.w1q[:, 128 * b:128 * b + 128], T.w1p[:, 128 * b:128 * b + 128], T.w1s[:, 512 * b:512 * b + 512]).then_inc(S["q_w%d" % b], 1)
+        v.wait_ge(S.ld_xn, 16)
+        v.quantize_mx(T.xnq[:], T.xnp[:], T.xn[:]).then_inc(S.q_xn, 1)
         act_v(T.hf, 3, 3, S.m_f3, S.a_f)
         v.wait_ge(S.a_f, 4)
         v.quantize_mx(T.fq[:, SIDE:SIDE + HALF], T.fp[:, SIDE:SIDE + HALF], T.hf[:]).then_inc(S.q_hf, 1)
-        v.wait_ge(S.ld_xn, 16)
-        v.quantize_mx(T.xnq[:], T.xnp[:], T.xn[:]).then_inc(S.q_xn, 1)
         act_v(T.hn, 5, 1, S.m_n1, S.a_n)
         act_v(T.hn, 7, 3, S.m_n3, S.a_n)
         v.wait_ge(S.a_n, 4)
@@ -224,30 +219,43 @@ def rank_program(g, core, T, topo):
         v.wait_ge(S.ld_v, 16)
         v.quantize_mx(T.w2q[:], T.w2p[:], T.w2s[:]).then_inc(S.q_v, 1)
         v.wait_ge(S.m_far, 1)
-        far_pc = _pieces([T.rank_of(far[j]) for j in _slot(Q, q)[0]])
-        for p, e, blk in far_pc:
-            v.tensor_copy(T.ys[:, RUN * blk:RUN * (blk + e - p)], ps[:, 2 * BANK + RUN * p:2 * BANK + RUN * e]).then_inc(S.e_far, 1)
+        b0 = T.rank_of(far[0])
+        land = [T.rank_of(far[j]) for j in _slot(Q, q)[0]]
+        parts = []
+        for part in range(2):
+            n = 0
+            for p, e, blk in _pieces([b if (b - b0) // (L // 2) == part else -9 * k - 9 for k, b in enumerate(land)]):
+                if blk >= 0:
+                    v.tensor_copy(T.ys[:, RUN * blk:RUN * (blk + e - p)], ps[:, 2 * BANK + RUN * p:2 * BANK + RUN * e]).then_inc(S["e_f%d" % part], 1)
+                    n += 1
+            parts.append(n)
 
-        c0, c1 = RUN * T.rank_of(mem[0]), RUN * T.rank_of(far[0])
+        c0, c1, wd = RUN * T.rank_of(mem[0]), RUN * b0, HALF // 2
         sy.wait_ge(S.e_near, 1 + len(near_pc))
         sy.dma_start(T.y[:, c0:c0 + HALF], T.ys[:, c0:c0 + HALF]).then_inc(S.st, 16)
-        sy.wait_ge(S.e_far, len(far_pc))
-        sy.dma_start(T.y[:, c1:c1 + HALF], T.ys[:, c1:c1 + HALF]).then_inc(S.st, 16)
+        sy.wait_ge(S.e_f0, parts[0])
+        sy.dma_start(T.y[:, c1:c1 + wd], T.ys[:, c1:c1 + wd]).then_inc(S.st, 16)
         sy.wait_ge(S.st, 32)
+        sc.wait_ge(S.e_f1, parts[1])
+        sc.dma_start(T.y[:, c1 + wd:c1 + HALF], T.ys[:, c1 + wd:c1 + HALF]).then_inc(S.st_b, 16)
+        sc.wait_ge(S.st_b, 16)
 
-        seen = []
+        g.wait_ge(S.q_hf, 1)
+        waited = False
         for call in _calls(P, topo, core):
-            if call[0][1] not in seen:
-                seen.append(call[0][1])
-                g.wait_ge(S.q_hf if call[0][1] == "far" else S.q_hn, 1)
+            if call[0][1] == "near" and not waited:
+                waited = True
+                g.wait_ge(S.q_hn, 1)
             items = []
             for d, tag, kind, i, es in call:
-                if tag == "far":
-                    order, base, bq, bp = _slot(P, i)
-                    a, c, sq, sp = SIDE + RUN * ford.index(i), base + RUN * order.index(q), T.fq, T.fp
-                    sem = S.gat_q if kind == "q" else S.gat_p
-                else:
+                if tag == "near":
                     a, c, bq, bp, sq, sp, sem = RUN * i, RUN * (q if q < i else q - 1), "lnq", "lnp", T.nq, T.npl, S.near_arr
+                else:
+                    order, base, bq, bp = _slot(P, i)
+                    a, c, sq, sp = SIDE + RUN * i, base + RUN * order.index(q), T.fq, T.fp
+                    sem = S.gat_q if kind == "q" else S.gat_p
+                    if tag == "dir":
+                        c, bq, sem = RUN * order.index(q), "lfq", S.far_arr
                 if kind == "q":
                     items.append((d, T[bq][:, c:c + RUN].bitcast(u8), sq[:, a:a + RUN].bitcast(u8), sem, es))
                 else:
@@ -255,15 +263,15 @@ def rank_program(g, core, T, topo):
             sent += _fan(g, topo, items, S.sent)
 
     if gate:
-        other = [s for s in mem if s != core][0]
-        kinds = [call[0][2] for call in _calls(P, topo, other) if call[0][1] == "far" and core in [it[0] for it in call]]
-        for kind in kinds:
+        for kind in ("q", "p"):
             g.wait_ge(S.gat_q if kind == "q" else S.gat_p, _due(P, topo, core, "far", kind))
             items = []
             for i, es in _cross(P, topo, core):
                 _, base, bq, bp = _slot(P, i)
                 if kind == "q":
-                    items.append((far[i], T.lfq[:].bitcast(u8), T[bq][:, base:base + HALF].bitcast(u8), S.far_arr, es))
+                    lo, hi = _held(P, i)
+                    items.append((far[i], T.lfq[:, RUN * lo:RUN * hi].bitcast(u8),
+                                  T[bq][:, base + RUN * lo:base + RUN * hi].bitcast(u8), S.far_arr, es))
                 else:
                     items.append((far[i], T.lfp[:], T[bp][:, base:base + HALF], S.far_arr, es))
             sent += _fan(g, topo, items, S.sent)

@@ -7,31 +7,34 @@ RUN = NC // N
 HALF = NC // 2
 SIDE = HALF - RUN
 L = HALF // RUN
+PC = 128
+NP = NC // PC
+OWN0 = PC - 2 * RUN
+OWN1 = RUN - OWN0
+HEAD = PC - 2 * RUN - OWN1
 CONST = 0.031
 BANK = 512
-W1_PARTS = 4
 
 CODE, PLANE, BF = "float8_e4m3fn_x4", "uint8", "bfloat16"
 SCRATCH = {
-    "xf": ("sbuf", [128, 4 * HALF], BF), "xn": ("sbuf", [128, 4 * HALF], BF),
-    "w1s": ("sbuf", [128, 4 * 512], BF), "w2s": ("sbuf", [128, 512], BF),
-    "xfq": ("sbuf", [128, HALF], CODE), "xfp": ("sbuf", [128, HALF], PLANE),
-    "xnq": ("sbuf", [128, HALF], CODE), "xnp": ("sbuf", [128, HALF], PLANE),
+    "xs": ("sbuf", [128, 4 * NC], BF), "w1s": ("sbuf", [128, 4 * 512], BF), "w2s": ("sbuf", [128, 512], BF),
+    "xq": ("sbuf", [128, NC], CODE), "xp": ("sbuf", [128, NC], PLANE),
     "w1q": ("sbuf", [128, 512], CODE), "w1p": ("sbuf", [128, 512], PLANE),
     "w2q": ("sbuf", [128, 128], CODE), "w2p": ("sbuf", [128, 128], PLANE),
-    "hf": ("sbuf", [128, 4 * HALF], BF), "hn": ("sbuf", [128, 4 * HALF], BF),
-    "fq": ("sbuf", [128, SIDE + HALF + SIDE], CODE), "fp": ("sbuf", [128, SIDE + HALF + SIDE], PLANE),
-    "nq": ("sbuf", [128, HALF], CODE), "npl": ("sbuf", [128, HALF], PLANE),
+    "hs": ("sbuf", [128, 4 * NC], BF),
+    "aq": ("sbuf", [128, PC], CODE), "ap": ("sbuf", [128, PC], PLANE),
+    "fq": ("sbuf", [128, SIDE + 2 * PC], CODE), "fp": ("sbuf", [128, SIDE + 2 * PC], PLANE),
     "gq": ("sbuf", [128, HALF], CODE), "gp": ("sbuf", [128, HALF], PLANE),
-    "lnq": ("sbuf", [128, SIDE], CODE), "lnp": ("sbuf", [128, SIDE], PLANE),
-    "lfq": ("sbuf", [128, HALF], CODE), "lfp": ("sbuf", [128, HALF], PLANE),
+    "lq": ("sbuf", [128, SIDE + HALF], CODE), "lp": ("sbuf", [128, SIDE + HALF], PLANE),
     "ys": ("sbuf", [128, NC], "float32"),
     "ps": ("psum", [128, 8 * BANK], "float32"),
 }
-SEMAPHORES = (["ld_xf", "ld_xn", "ld_v", "q_xf", "q_xn", "q_v", "q_hf", "q_hn", "a_f", "a_n", "m_own", "m_near", "m_far",
-               "e_near", "e_f0", "e_f1", "st", "st_b", "near_arr", "far_arr", "gat_q", "gat_p", "sent"]
+SEMAPHORES = (["ld_v", "q_v", "m_own0", "m_own1", "m_near", "m_early", "m_far",
+               "e_near", "e_early", "e_late", "st", "st_b", "near_arr", "far_e", "far_l", "gat_q", "gat_p", "sent"]
               + ["ld_w%d" % i for i in range(4)] + ["q_w%d" % i for i in range(4)]
-              + ["m_f%d" % i for i in range(4)] + ["m_n%d" % i for i in range(4)])
+              + ["ld_x%d" % i for i in range(NP)] + ["q_x%d" % i for i in range(NP)]
+              + ["a_%d" % i for i in range(NP)] + ["q_h%d" % i for i in range(NP)]
+              + ["m%d_%d" % (i, b) for i in range(NP) for b in range(4)])
 
 
 def _bits(m):
@@ -48,9 +51,28 @@ def _plan(T, topo):
                  if topo.chip(c) == ch and all(topo.may_write(c, d) for d in far)]
         own = [c for c in ports if c in mem]
         aid = [c for c in ports if c not in mem]
-        gate = [(own[-1], "front"), (aid[0], "aid"), (aid[1], "aid"), (own[0], "back")]
+        gate = [(own[-1], "rank"), (aid[0], "aid"), (aid[1], "aid"), (own[0], "rank")]
         plan[ch] = {"mem": mem, "far": far, "gate": gate, "own": own}
     return plan
+
+
+def _tile(P, core):
+    q = P["mem"].index(core)
+    aid = [i for i in range(L) if P["gate"][i][1] == "aid"]
+    rk = sorted([i for i in range(L) if P["gate"][i][1] != "aid"], key=lambda i: P["gate"][i][0] != core)
+    cyc = [(q + k) % L for k in range(1, L)]
+    return ([("f", i, 0, RUN) for i in aid] + [("n", q, 0, OWN0)]
+            + [("f", i, 0, RUN) for i in rk] + [("n", q, OWN0, OWN1), ("n", cyc[0], 0, HEAD)]
+            + [("n", cyc[0], HEAD, RUN - HEAD)] + [("n", j, 0, RUN) for j in cyc[1:]])
+
+
+def _at(P, core, side, i):
+    t = 0
+    for s, k, a, n in _tile(P, core):
+        if (s, k, a) == (side, i, 0):
+            return ((t + RUN - 1) // PC, "aq", "ap", t) if t < PC else ((t + RUN - 1) // PC, "fq", "fp", SIDE + t - PC)
+        t += n
+    return None
 
 
 def _slot(P, i):
@@ -59,12 +81,9 @@ def _slot(P, i):
     plain = [j for j in range(L) if mem[j] not in P["own"]]
     port = [j for j in range(L) if mem[j] in P["own"]]
     if kind == "aid":
-        return plain + port, 0, "gq", "gp"
+        return port + plain, "gq", "gp"
     gl = mem.index(G)
-    rest = [j for j in port if j != gl]
-    if kind == "front":
-        return rest + plain + [gl], 0, "fq", "fp"
-    return [gl] + plain + rest, SIDE + HALF - RUN, "fq", "fp"
+    return [j for j in port if j != gl] + plain + [gl], "fq", "fp"
 
 
 def _held(P, i):
@@ -85,19 +104,20 @@ def _calls(P, topo, src):
     mem = P["mem"]
     near = [j for j in range(L) if mem[j] != src]
     on = _bits(topo.mask(src, mem[near[0]]))
-    todo = [i for i in range(L) if P["gate"][i][0] != src]
+    aid = [i for i in range(L) if P["gate"][i][1] == "aid"]
+    rk = [i for i in range(L) if P["gate"][i][1] != "aid" and P["gate"][i][0] != src]
     out = []
     if src in P["own"]:
         off = _bits(topo.mask(src, P["far"][0]))
         high = [e for e in on if e not in off]
-        out.append([(P["far"][i], "dir", "q", i, e) for i, e in zip(todo, _deal(len(todo), off, False))])
-        out.append([(P["gate"][i][0], "far", "p", i, e) for i, e in zip(todo, _deal(len(todo), high, False))])
+        for grp in (aid, rk):
+            out.append([(P["gate"][i][0], "far", "p", i, e) for i, e in zip(grp, _deal(len(grp), high, False))])
+            out.append([(P["far"][i], "dir", "q", i, e) for i, e in zip(grp, _deal(len(grp), off, False))])
     else:
-        aid = [i for i in todo if P["gate"][i][1] == "aid"]
-        own = [i for i in todo if P["gate"][i][1] != "aid"]
         h = len(on) // 2
-        for grp, kind, es in ((aid, "q", on[:h]), (own, "q", on[h:]), (aid + own, "p", on)):
-            out.append([(P["gate"][i][0], "far", kind, i, e) for i, e in zip(grp, _deal(len(grp), es, kind == "p"))])
+        for grp, es in ((aid, on[:h]), (rk, on[h:])):
+            for kind in "pq":
+                out.append([(P["gate"][i][0], "far", kind, i, e) for i, e in zip(grp, _deal(len(grp), es, False))])
     for kind in ("q", "p"):
         out.append([(mem[j], "near", kind, j, e) for j, e in zip(near, _deal(len(near), on, kind == "p"))])
     return out
@@ -154,125 +174,164 @@ def rank_program(g, core, T, topo):
         q = mem.index(core)
         ps = T.ps
 
-        c0 = 4 * RUN * T.rank_of(far[0])
-        sy.dma_start(T.xf[:], T.x[:, c0:c0 + 4 * HALF]).then_inc(S.ld_xf, 16)
-        wid = 4 * 512 // W1_PARTS
-        for n in range(W1_PARTS):
-            (sc if n % 2 == 0 else sy).dma_start(T.w1s[:, wid * n:wid * (n + 1)], T.w1[:, wid * n:wid * (n + 1)]).then_inc(S["ld_w%d" % n], 16)
-        c0 = 4 * RUN * T.rank_of(mem[0])
-        sc.dma_start(T.xn[:], T.x[:, c0:c0 + 4 * HALF]).then_inc(S.ld_xn, 16)
+        stretch, t = [], 0
+        for s, k, a, n in _tile(P, core):
+            c = RUN * T.rank_of(far[k] if s == "f" else mem[k]) + a
+            if stretch and t % PC and stretch[-1][1] + stretch[-1][2] == c:
+                stretch[-1][2] += n
+            else:
+                stretch.append([t, c, n])
+            t += n
+        xl = [[z for z in stretch if z[0] // PC == pc] for pc in range(NP)]
+
+        def load_x(eng, z):
+            eng.dma_start(T.xs[:, 4 * z[0]:4 * (z[0] + z[2])], T.x[:, 4 * z[1]:4 * (z[1] + z[2])]).then_inc(S["ld_x%d" % (z[0] // PC)], 16)
+
+        turn = 0
+        for z in xl[0]:
+            load_x(sc if turn % 2 else sy, z)
+            turn += 1
+        for n in range(4):
+            (sc if turn % 2 else sy).dma_start(T.w1s[:, 512 * n:512 * (n + 1)], T.w1[:, 512 * n:512 * (n + 1)]).then_inc(S["ld_w%d" % n], 16)
+            turn += 1
+        for z in xl[1] + xl[2]:
+            load_x(sy, z)
         sy.dma_start(T.w2s[:], T.w2[:]).then_inc(S.ld_v, 16)
 
-        for half, (xq, xp, sx, tag) in enumerate(((T.xfq, T.xfp, S.q_xf, "m_f%d"), (T.xnq, T.xnp, S.q_xn, "m_n%d"))):
-            pe.wait_ge(sx, 1)
+        for pc in range(NP):
+            pe.wait_ge(S["q_x%d" % pc], 1)
+            if pc == 2:
+                pe.wait_ge(S.a_0, 4)
             for b in range(4):
-                if half == 0:
+                if pc == 0:
                     pe.wait_ge(S["q_w%d" % b], 1)
-                k = 4 * half + b
-                pe.matmul_mx(ps[:, BANK * k:BANK * k + HALF], T.w1q[:, 128 * b:128 * b + 128], T.w1p[:, 128 * b:128 * b + 128],
-                             xq[:], xp[:], True, True).then_inc(S[tag % b], 1)
-        win = 0 if RUN * q + RUN <= 128 else HALF - 128
-        pe.wait_ge(S.a_f, 4)
-        pe.wait_ge(S.q_hn, 1)
+                k = (4 * pc + b) % 8
+                pe.matmul_mx(ps[:, BANK * k:BANK * k + PC], T.w1q[:, 128 * b:128 * b + 128], T.w1p[:, 128 * b:128 * b + 128],
+                             T.xq[:, PC * pc:PC * pc + PC], T.xp[:, PC * pc:PC * pc + PC], True, True).then_inc(S["m%d_%d" % (pc, b)], 1)
+        pe.wait_ge(S.a_1, 4)
         pe.wait_ge(S.q_v, 1)
-        pe.matmul_mx(ps[:, 0:128], T.w2q[:], T.w2p[:], T.nq[:, win:win + 128], T.npl[:, win:win + 128], True, True).then_inc(S.m_own, 1)
+        pe.wait_ge(S.q_h0, 1)
+        pe.matmul_mx(ps[:, 4 * BANK:4 * BANK + PC], T.w2q[:], T.w2p[:], T.aq[:], T.ap[:], True, True).then_inc(S.m_own0, 1)
+        pe.wait_ge(S.q_h1, 1)
+        pe.matmul_mx(ps[:, 5 * BANK:5 * BANK + PC], T.w2q[:], T.w2p[:], T.fq[:, SIDE:SIDE + PC], T.fp[:, SIDE:SIDE + PC], True, True).then_inc(S.m_own1, 1)
         pe.wait_ge(S.near_arr, _due(P, topo, core, "near", "qp"))
-        pe.matmul_mx(ps[:, BANK:BANK + SIDE], T.w2q[:], T.w2p[:], T.lnq[:], T.lnp[:], True, True).then_inc(S.m_near, 1)
-        pe.wait_ge(S.far_arr, 2 * sum(len(es) for i, es in _cross(Q, topo, Q["gate"][q][0]) if i == q) + _due(Q, topo, core, "dir", "q"))
-        pe.matmul_mx(ps[:, 2 * BANK:2 * BANK + HALF], T.w2q[:], T.w2p[:], T.lfq[:], T.lfp[:], True, True).then_inc(S.m_far, 1)
+        pe.matmul_mx(ps[:, 6 * BANK:6 * BANK + SIDE], T.w2q[:], T.w2p[:], T.lq[:, 0:SIDE], T.lp[:, 0:SIDE], True, True).then_inc(S.m_near, 1)
+        lo = _held(Q, q)[0]
+        blocks = [T.rank_of(far[j]) for j in _slot(Q, q)[0]]
+        ncross = sum(len(es) for i, es in _cross(Q, topo, Q["gate"][q][0]) if i == q)
+        se = SIDE + RUN * lo - PC
+        wl = max(PC, RUN * (L - lo))
+        sl = SIDE + HALF - wl
+        pe.wait_ge(S.a_2, 4)
+        pe.wait_ge(S.far_e, ncross + _due(Q, topo, core, "dir", "q"))
+        pe.matmul_mx(ps[:, 0:PC], T.w2q[:], T.w2p[:], T.lq[:, se:se + PC], T.lp[:, se:se + PC], True, True).then_inc(S.m_early, 1)
+        pe.wait_ge(S.far_l, ncross)
+        pe.matmul_mx(ps[:, 7 * BANK:7 * BANK + wl], T.w2q[:], T.w2p[:], T.lq[:, sl:sl + wl], T.lp[:, sl:sl + wl], True, True).then_inc(S.m_far, 1)
 
-        def act_s(h, k, b, sm, sa):
-            sc.wait_ge(sm, 1)
-            sc.activation(h[:, b:4 * HALF:4], ps[:, BANK * k:BANK * k + HALF], ActivationFunctionType.Relu, scale=CONST).then_inc(sa, 1)
+        def views(pc, b):
+            k = (4 * pc + b) % 8
+            return T.hs[:, 4 * PC * pc + b:4 * PC * (pc + 1):4], ps[:, BANK * k:BANK * k + PC]
 
-        def act_v(h, k, b, sm, sa):
-            v.wait_ge(sm, 1)
-            v.tensor_scalar(h[:, b:4 * HALF:4], ps[:, BANK * k:BANK * k + HALF], 0.0, CONST, AluOpType.max, AluOpType.mult).then_inc(sa, 1)
-
-        for b in (0, 1, 2):
-            act_s(T.hf, b, b, S["m_f%d" % b], S.a_f)
-        for b in (0, 2):
-            act_s(T.hn, 4 + b, b, S["m_n%d" % b], S.a_n)
-        sc.wait_ge(S.m_own, 1)
-        o = RUN * q - win
-        sc.activation(T.ys[:, RUN * rank:RUN * rank + RUN], ps[:, o:o + RUN], ActivationFunctionType.Copy).then_inc(S.e_near, 1)
+        for pc in range(NP):
+            for b in range(4 if pc == 0 else 3):
+                o, i_ = views(pc, b)
+                sc.wait_ge(S["m%d_%d" % (pc, b)], 1)
+                sc.activation(o, i_, ActivationFunctionType.Relu, scale=CONST).then_inc(S["a_%d" % pc], 1)
+        y0 = RUN * rank
+        sc.wait_ge(S.m_own0, 1)
+        sc.activation(T.ys[:, y0:y0 + OWN0], ps[:, 4 * BANK + 2 * RUN:4 * BANK + PC], ActivationFunctionType.Copy).then_inc(S.e_near, 1)
+        sc.wait_ge(S.m_own1, 1)
+        sc.activation(T.ys[:, y0 + OWN0:y0 + RUN], ps[:, 5 * BANK + 2 * RUN:5 * BANK + 2 * RUN + OWN1], ActivationFunctionType.Copy).then_inc(S.e_near, 1)
         sc.wait_ge(S.m_near, 1)
         near_pc = _pieces([T.rank_of(mem[j]) for j in range(L) if j != q])
         for p, e, blk in near_pc:
-            sc.activation(T.ys[:, RUN * blk:RUN * (blk + e - p)], ps[:, BANK + RUN * p:BANK + RUN * e], ActivationFunctionType.Copy).then_inc(S.e_near, 1)
+            sc.activation(T.ys[:, RUN * blk:RUN * (blk + e - p)], ps[:, 6 * BANK + RUN * p:6 * BANK + RUN * e], ActivationFunctionType.Copy).then_inc(S.e_near, 1)
+        sc.wait_ge(S.m_early, 1)
+        early_pc = _pieces(blocks[:lo])
+        for p, e, blk in early_pc:
+            sc.activation(T.ys[:, RUN * blk:RUN * (blk + e - p)], ps[:, PC - RUN * (lo - p):PC - RUN * (lo - e)], ActivationFunctionType.Copy).then_inc(S.e_early, 1)
 
-        v.wait_ge(S.ld_xf, 16)
-        v.quantize_mx(T.xfq[:], T.xfp[:], T.xf[:]).then_inc(S.q_xf, 1)
+        def quant_x(pc):
+            v.wait_ge(S["ld_x%d" % pc], 16 * len(xl[pc]))
+            v.quantize_mx(T.xq[:, PC * pc:PC * pc + PC], T.xp[:, PC * pc:PC * pc + PC], T.xs[:, 4 * PC * pc:4 * PC * (pc + 1)]).then_inc(S["q_x%d" % pc], 1)
+
+        def quant_h(pc):
+            oq, op = (T.aq[:], T.ap[:]) if pc == 0 else (T.fq[:, SIDE + PC * (pc - 1):SIDE + PC * pc], T.fp[:, SIDE + PC * (pc - 1):SIDE + PC * pc])
+            v.wait_ge(S["a_%d" % pc], 4)
+            v.quantize_mx(oq, op, T.hs[:, 4 * PC * pc:4 * PC * (pc + 1)]).then_inc(S["q_h%d" % pc], 1)
+
+        def act_v(pc, b):
+            o, i_ = views(pc, b)
+            v.wait_ge(S["m%d_%d" % (pc, b)], 1)
+            v.tensor_scalar(o, i_, 0.0, CONST, AluOpType.max, AluOpType.mult).then_inc(S["a_%d" % pc], 1)
+
+        quant_x(0)
         for b in range(4):
-            if b % (4 // W1_PARTS) == 0:
-                v.wait_ge(S["ld_w%d" % (b // (4 // W1_PARTS))], 16)
+            v.wait_ge(S["ld_w%d" % b], 16)
             v.quantize_mx(T.w1q[:, 128 * b:128 * b + 128], T.w1p[:, 128 * b:128 * b + 128], T.w1s[:, 512 * b:512 * b + 512]).then_inc(S["q_w%d" % b], 1)
-        v.wait_ge(S.ld_xn, 16)
-        v.quantize_mx(T.xnq[:], T.xnp[:], T.xn[:]).then_inc(S.q_xn, 1)
-        act_v(T.hf, 3, 3, S.m_f3, S.a_f)
-        v.wait_ge(S.a_f, 4)
-        v.quantize_mx(T.fq[:, SIDE:SIDE + HALF], T.fp[:, SIDE:SIDE + HALF], T.hf[:]).then_inc(S.q_hf, 1)
-        act_v(T.hn, 5, 1, S.m_n1, S.a_n)
-        act_v(T.hn, 7, 3, S.m_n3, S.a_n)
-        v.wait_ge(S.a_n, 4)
-        v.quantize_mx(T.nq[:], T.npl[:], T.hn[:]).then_inc(S.q_hn, 1)
+        quant_x(1)
+        quant_h(0)
+        quant_x(2)
+        act_v(1, 3)
+        quant_h(1)
+        act_v(2, 3)
+        quant_h(2)
         v.wait_ge(S.ld_v, 16)
         v.quantize_mx(T.w2q[:], T.w2p[:], T.w2s[:]).then_inc(S.q_v, 1)
         v.wait_ge(S.m_far, 1)
-        b0 = T.rank_of(far[0])
-        land = [T.rank_of(far[j]) for j in _slot(Q, q)[0]]
-        parts = []
-        for part in range(2):
-            n = 0
-            for p, e, blk in _pieces([b if (b - b0) // (L // 2) == part else -9 * k - 9 for k, b in enumerate(land)]):
-                if blk >= 0:
-                    v.tensor_copy(T.ys[:, RUN * blk:RUN * (blk + e - p)], ps[:, 2 * BANK + RUN * p:2 * BANK + RUN * e]).then_inc(S["e_f%d" % part], 1)
-                    n += 1
-            parts.append(n)
+        late_pc = _pieces(blocks[lo:])
+        off = 7 * BANK + wl - RUN * (L - lo)
+        for p, e, blk in late_pc:
+            v.tensor_copy(T.ys[:, RUN * blk:RUN * (blk + e - p)], ps[:, off + RUN * p:off + RUN * e]).then_inc(S.e_late, 1)
 
-        c0, c1, wd = RUN * T.rank_of(mem[0]), RUN * b0, HALF // 2
-        sy.wait_ge(S.e_near, 1 + len(near_pc))
+        c0 = RUN * T.rank_of(mem[0])
+        l0, l1 = min(blocks[lo:]), max(blocks[lo:]) + 1
+        outside = _pieces(sorted(b for b in blocks[:lo] if not l0 <= b < l1))
+        sy.wait_ge(S.e_near, 2 + len(near_pc))
         sy.dma_start(T.y[:, c0:c0 + HALF], T.ys[:, c0:c0 + HALF]).then_inc(S.st, 16)
-        sy.wait_ge(S.e_f0, parts[0])
-        sy.dma_start(T.y[:, c1:c1 + wd], T.ys[:, c1:c1 + wd]).then_inc(S.st, 16)
-        sy.wait_ge(S.st, 32)
-        sc.wait_ge(S.e_f1, parts[1])
-        sc.dma_start(T.y[:, c1 + wd:c1 + HALF], T.ys[:, c1 + wd:c1 + HALF]).then_inc(S.st_b, 16)
+        if outside:
+            sy.wait_ge(S.e_early, len(early_pc))
+        for p, e, blk in outside:
+            sy.dma_start(T.y[:, RUN * blk:RUN * (blk + e - p)], T.ys[:, RUN * blk:RUN * (blk + e - p)]).then_inc(S.st, 16)
+        sy.wait_ge(S.st, 16 * (1 + len(outside)))
+        sc.wait_ge(S.e_early, len(early_pc))
+        sc.wait_ge(S.e_late, len(late_pc))
+        sc.dma_start(T.y[:, RUN * l0:RUN * l1], T.ys[:, RUN * l0:RUN * l1]).then_inc(S.st_b, 16)
         sc.wait_ge(S.st_b, 16)
 
-        g.wait_ge(S.q_hf, 1)
-        waited = False
+        have = -1
         for call in _calls(P, topo, core):
-            if call[0][1] == "near" and not waited:
-                waited = True
-                g.wait_ge(S.q_hn, 1)
             items = []
             for d, tag, kind, i, es in call:
+                pc, sq, sp, a = _at(P, core, "n" if tag == "near" else "f", i)
+                while have < pc:
+                    have += 1
+                    g.wait_ge(S["q_h%d" % have], 1)
                 if tag == "near":
-                    a, c, bq, bp, sq, sp, sem = RUN * i, RUN * (q if q < i else q - 1), "lnq", "lnp", T.nq, T.npl, S.near_arr
+                    c, bq, bp, sem = RUN * (q if q < i else q - 1), "lq", "lp", S.near_arr
                 else:
-                    order, base, bq, bp = _slot(P, i)
-                    a, c, sq, sp = SIDE + RUN * i, base + RUN * order.index(q), T.fq, T.fp
+                    order, bq, bp = _slot(P, i)
+                    c = RUN * order.index(q)
                     sem = S.gat_q if kind == "q" else S.gat_p
                     if tag == "dir":
-                        c, bq, sem = RUN * order.index(q), "lfq", S.far_arr
+                        c, bq, sem = SIDE + c, "lq", S.far_e
                 if kind == "q":
-                    items.append((d, T[bq][:, c:c + RUN].bitcast(u8), sq[:, a:a + RUN].bitcast(u8), sem, es))
+                    items.append((d, T[bq][:, c:c + RUN].bitcast(u8), T[sq][:, a:a + RUN].bitcast(u8), sem, es))
                 else:
-                    items.append((d, T[bp][:, c:c + RUN], sp[:, a:a + RUN], sem, es))
+                    items.append((d, T[bp][:, c:c + RUN], T[sp][:, a:a + RUN], sem, es))
             sent += _fan(g, topo, items, S.sent)
 
     if gate:
-        for kind in ("q", "p"):
+        for kind in "pq":
             g.wait_ge(S.gat_q if kind == "q" else S.gat_p, _due(P, topo, core, "far", kind))
             items = []
             for i, es in _cross(P, topo, core):
-                _, base, bq, bp = _slot(P, i)
+                _, bq, bp = _slot(P, i)
                 if kind == "q":
                     lo, hi = _held(P, i)
-                    items.append((far[i], T.lfq[:, RUN * lo:RUN * hi].bitcast(u8),
-                                  T[bq][:, base + RUN * lo:base + RUN * hi].bitcast(u8), S.far_arr, es))
+                    items.append((far[i], T.lq[:, SIDE + RUN * lo:SIDE + RUN * hi].bitcast(u8),
+                                  T[bq][:, RUN * lo:RUN * hi].bitcast(u8), S.far_l, es))
                 else:
-                    items.append((far[i], T.lfp[:], T[bp][:, base:base + HALF], S.far_arr, es))
+                    items.append((far[i], T.lp[:, SIDE:SIDE + HALF], T[bp][:, 0:HALF], S.far_e, es))
             sent += _fan(g, topo, items, S.sent)
     g.wait_ge(S.sent, sent)

from concourse.bass import DstId, RemoteDMATransfer
from concourse.mybir import dt, AluOpType, ActivationFunctionType

N = 8
NC = 384
RUN = NC // N
HALF = NC // 2
SIDE = HALF - RUN
L = HALF // RUN
PC = 128
NP = NC // PC
OWN0 = PC - 2 * RUN
OWN1 = RUN - OWN0
HEAD = PC - 2 * RUN - OWN1
CONST = 0.031
BANK = 512

CODE, PLANE, BF = "float8_e4m3fn_x4", "uint8", "bfloat16"
SCRATCH = {
    "xs": ("sbuf", [128, 4 * NC], BF), "w1s": ("sbuf", [128, 4 * 512], BF), "w2s": ("sbuf", [128, 512], BF),
    "xq": ("sbuf", [128, NC], CODE), "xp": ("sbuf", [128, NC], PLANE),
    "w1q": ("sbuf", [128, 512], CODE), "w1p": ("sbuf", [128, 512], PLANE),
    "w2q": ("sbuf", [128, 128], CODE), "w2p": ("sbuf", [128, 128], PLANE),
    "hs": ("sbuf", [128, 4 * NC], BF),
    "aq": ("sbuf", [128, PC], CODE), "ap": ("sbuf", [128, PC], PLANE),
    "fq": ("sbuf", [128, SIDE + 2 * PC], CODE), "fp": ("sbuf", [128, SIDE + 2 * PC], PLANE),
    "gq": ("sbuf", [128, HALF], CODE), "gp": ("sbuf", [128, HALF], PLANE),
    "lq": ("sbuf", [128, SIDE + HALF], CODE), "lp": ("sbuf", [128, SIDE + HALF], PLANE),
    "ys": ("sbuf", [128, NC], "float32"),
    "ps": ("psum", [128, 8 * BANK], "float32"),
}
SEMAPHORES = (["ld_v", "q_v", "m_own0", "m_own1", "m_near", "m_early", "m_far",
               "e_near", "e_early", "e_late", "st", "st_b", "near_arr", "far_e", "far_l", "gat_q", "gat_p", "sent"]
              + ["ld_w%d" % i for i in range(4)] + ["q_w%d" % i for i in range(4)]
              + ["ld_x%d" % i for i in range(NP)] + ["q_x%d" % i for i in range(NP)]
              + ["a_%d" % i for i in range(NP)] + ["q_h%d" % i for i in range(NP)]
              + ["m%d_%d" % (i, b) for i in range(NP) for b in range(4)])


def _bits(m):
    return [e for e in range(m.bit_length()) if (m >> e) & 1]


def _plan(T, topo):
    cores = list(T.cores)
    plan = {}
    for ch in sorted({topo.chip(c) for c in cores}):
        mem = [c for c in cores if topo.chip(c) == ch]
        far = [c for c in cores if topo.chip(c) != ch]
        ports = [c for c in range(topo.CORES_PER_CHIP * topo.CHIPS)
                 if topo.chip(c) == ch and all(topo.may_write(c, d) for d in far)]
        own = [c for c in ports if c in mem]
        aid = [c for c in ports if c not in mem]
        gate = [(own[-1], "rank"), (aid[0], "aid"), (aid[1], "aid"), (own[0], "rank")]
        plan[ch] = {"mem": mem, "far": far, "gate": gate, "own": own}
    return plan


def _tile(P, core):
    q = P["mem"].index(core)
    aid = [i for i in range(L) if P["gate"][i][1] == "aid"]
    rk = sorted([i for i in range(L) if P["gate"][i][1] != "aid"], key=lambda i: P["gate"][i][0] != core)
    cyc = [(q + k) % L for k in range(1, L)]
    return ([("f", i, 0, RUN) for i in aid] + [("n", q, 0, OWN0)]
            + [("f", i, 0, RUN) for i in rk] + [("n", q, OWN0, OWN1), ("n", cyc[0], 0, HEAD)]
            + [("n", cyc[0], HEAD, RUN - HEAD)] + [("n", j, 0, RUN) for j in cyc[1:]])


def _at(P, core, side, i):
    t = 0
    for s, k, a, n in _tile(P, core):
        if (s, k, a) == (side, i, 0):
            return ((t + RUN - 1) // PC, "aq", "ap", t) if t < PC else ((t + RUN - 1) // PC, "fq", "fp", SIDE + t - PC)
        t += n
    return None


def _slot(P, i):
    G, kind = P["gate"][i]
    mem = P["mem"]
    plain = [j for j in range(L) if mem[j] not in P["own"]]
    port = [j for j in range(L) if mem[j] in P["own"]]
    if kind == "aid":
        return port + plain, "gq", "gp"
    gl = mem.index(G)
    return [j for j in port if j != gl] + plain + [gl], "fq", "fp"


def _held(P, i):
    G = P["gate"][i][0]
    have = [k for k, j in enumerate(_slot(P, i)[0]) if P["mem"][j] not in P["own"] or P["mem"][j] == G]
    return have[0], have[-1] + 1


def _deal(n, es, turn):
    if n == 3:
        k = len(es) // 4
        return [es[2 * k:3 * k], es[3 * k:], es[:2 * k]] if turn else [es[:k], es[k:2 * k], es[2 * k:]]
    k = len(es) // n
    return [es[k * i:k * i + k] for i in range(n)]


def _calls(P, topo, src):
    mem = P["mem"]
    near = [j for j in range(L) if mem[j] != src]
    on = _bits(topo.mask(src, mem[near[0]]))
    aid = [i for i in range(L) if P["gate"][i][1] == "aid"]
    rk = [i for i in range(L) if P["gate"][i][1] != "aid" and P["gate"][i][0] != src]
    out = []
    if src in P["own"]:
        off = _bits(topo.mask(src, P["far"][0]))
        high = [e for e in on if e not in off]
        for grp in (aid, rk):
            out.append([(P["gate"][i][0], "far", "p", i, e) for i, e in zip(grp, _deal(len(grp), high, False))])
            out.append([(P["far"][i], "dir", "q", i, e) for i, e in zip(grp, _deal(len(grp), off, False))])
    else:
        h = len(on) // 2
        for grp, es in ((aid, on[:h]), (rk, on[h:])):
            for kind in "pq":
                out.append([(P["gate"][i][0], "far", kind, i, e) for i, e in zip(grp, _deal(len(grp), es, False))])
    for kind in ("q", "p"):
        out.append([(mem[j], "near", kind, j, e) for j, e in zip(near, _deal(len(near), on, kind == "p"))])
    return out


def _due(P, topo, dst, tag, kinds):
    return sum(len(it[4]) for s in P["mem"] for call in _calls(P, topo, s) for it in call
               if it[0] == dst and it[1] == tag and it[2] in kinds)


def _cross(P, topo, G):
    serves = [i for i in range(L) if P["gate"][i][0] == G]
    return list(zip(serves, _deal(len(serves), _bits(topo.mask(G, P["far"][serves[0]])), False)))


def _pieces(blocks):
    out, p = [], 0
    while p < len(blocks):
        e = p + 1
        while e < len(blocks) and blocks[e] == blocks[e - 1] + 1:
            e += 1
        out.append((p, e, blocks[p]))
        p = e
    return out


def _fan(g, topo, items, local_sem):
    trs = []
    for d, dst, src, sem, es in items:
        rid, pid, _ = topo.addr(d)
        trs.append(RemoteDMATransfer(dst_ids=[DstId(rid=rid, pnc=pid)], dma_engine_mask=sum(1 << e for e in es),
                                     remote_sem=sem, src=src, dst=dst))
    g.remote_dma_fused(trs, local_sem=local_sem)
    return sum(len(it[4]) for it in items)


def rank_program(g, core, T, topo):
    S = T.sem
    plan = _plan(T, topo)
    if topo.chip(core) not in plan:
        return
    P = plan[topo.chip(core)]
    mem, far = P["mem"], P["far"]
    rank = T.rank_of(core)
    gate = core in [G for G, _ in P["gate"]]
    if rank is None and not gate:
        return
    u8 = dt.uint8
    sent = 0

    if rank is not None:
        sy, sc, v, pe = g.sync, g.scalar, g.vector, g.tensor
        Q = plan[topo.chip(far[0])]
        q = mem.index(core)
        ps = T.ps

        stretch, t = [], 0
        for s, k, a, n in _tile(P, core):
            c = RUN * T.rank_of(far[k] if s == "f" else mem[k]) + a
            if stretch and t % PC and stretch[-1][1] + stretch[-1][2] == c:
                stretch[-1][2] += n
            else:
                stretch.append([t, c, n])
            t += n
        xl = [[z for z in stretch if z[0] // PC == pc] for pc in range(NP)]

        def load_x(eng, z):
            eng.dma_start(T.xs[:, 4 * z[0]:4 * (z[0] + z[2])], T.x[:, 4 * z[1]:4 * (z[1] + z[2])]).then_inc(S["ld_x%d" % (z[0] // PC)], 16)

        turn = 0
        for z in xl[0]:
            load_x(sc if turn % 2 else sy, z)
            turn += 1
        for n in range(4):
            (sc if turn % 2 else sy).dma_start(T.w1s[:, 512 * n:512 * (n + 1)], T.w1[:, 512 * n:512 * (n + 1)]).then_inc(S["ld_w%d" % n], 16)
            turn += 1
        for z in xl[1] + xl[2]:
            load_x(sy, z)
        sy.dma_start(T.w2s[:], T.w2[:]).then_inc(S.ld_v, 16)

        for pc in range(NP):
            pe.wait_ge(S["q_x%d" % pc], 1)
            if pc == 2:
                pe.wait_ge(S.a_0, 4)
            for b in range(4):
                if pc == 0:
                    pe.wait_ge(S["q_w%d" % b], 1)
                k = (4 * pc + b) % 8
                pe.matmul_mx(ps[:, BANK * k:BANK * k + PC], T.w1q[:, 128 * b:128 * b + 128], T.w1p[:, 128 * b:128 * b + 128],
                             T.xq[:, PC * pc:PC * pc + PC], T.xp[:, PC * pc:PC * pc + PC], True, True).then_inc(S["m%d_%d" % (pc, b)], 1)
        pe.wait_ge(S.a_1, 4)
        pe.wait_ge(S.q_v, 1)
        pe.wait_ge(S.q_h0, 1)
        pe.matmul_mx(ps[:, 4 * BANK:4 * BANK + PC], T.w2q[:], T.w2p[:], T.aq[:], T.ap[:], True, True).then_inc(S.m_own0, 1)
        pe.wait_ge(S.q_h1, 1)
        pe.matmul_mx(ps[:, 5 * BANK:5 * BANK + PC], T.w2q[:], T.w2p[:], T.fq[:, SIDE:SIDE + PC], T.fp[:, SIDE:SIDE + PC], True, True).then_inc(S.m_own1, 1)
        pe.wait_ge(S.near_arr, _due(P, topo, core, "near", "qp"))
        pe.matmul_mx(ps[:, 6 * BANK:6 * BANK + SIDE], T.w2q[:], T.w2p[:], T.lq[:, 0:SIDE], T.lp[:, 0:SIDE], True, True).then_inc(S.m_near, 1)
        lo = _held(Q, q)[0]
        blocks = [T.rank_of(far[j]) for j in _slot(Q, q)[0]]
        ncross = sum(len(es) for i, es in _cross(Q, topo, Q["gate"][q][0]) if i == q)
        se = SIDE + RUN * lo - PC
        wl = max(PC, RUN * (L - lo))
        sl = SIDE + HALF - wl
        pe.wait_ge(S.a_2, 4)
        pe.wait_ge(S.far_e, ncross + _due(Q, topo, core, "dir", "q"))
        pe.matmul_mx(ps[:, 0:PC], T.w2q[:], T.w2p[:], T.lq[:, se:se + PC], T.lp[:, se:se + PC], True, True).then_inc(S.m_early, 1)
        pe.wait_ge(S.far_l, ncross)
        pe.matmul_mx(ps[:, 7 * BANK:7 * BANK + wl], T.w2q[:], T.w2p[:], T.lq[:, sl:sl + wl], T.lp[:, sl:sl + wl], True, True).then_inc(S.m_far, 1)

        def views(pc, b):
            k = (4 * pc + b) % 8
            return T.hs[:, 4 * PC * pc + b:4 * PC * (pc + 1):4], ps[:, BANK * k:BANK * k + PC]

        for pc in range(NP):
            for b in range(4 if pc == 0 else 3):
                o, i_ = views(pc, b)
                sc.wait_ge(S["m%d_%d" % (pc, b)], 1)
                sc.activation(o, i_, ActivationFunctionType.Relu, scale=CONST).then_inc(S["a_%d" % pc], 1)
        y0 = RUN * rank
        sc.wait_ge(S.m_own0, 1)
        sc.activation(T.ys[:, y0:y0 + OWN0], ps[:, 4 * BANK + 2 * RUN:4 * BANK + PC], ActivationFunctionType.Copy).then_inc(S.e_near, 1)
        sc.wait_ge(S.m_own1, 1)
        sc.activation(T.ys[:, y0 + OWN0:y0 + RUN], ps[:, 5 * BANK + 2 * RUN:5 * BANK + 2 * RUN + OWN1], ActivationFunctionType.Copy).then_inc(S.e_near, 1)
        sc.wait_ge(S.m_near, 1)
        near_pc = _pieces([T.rank_of(mem[j]) for j in range(L) if j != q])
        for p, e, blk in near_pc:
            sc.activation(T.ys[:, RUN * blk:RUN * (blk + e - p)], ps[:, 6 * BANK + RUN * p:6 * BANK + RUN * e], ActivationFunctionType.Copy).then_inc(S.e_near, 1)
        sc.wait_ge(S.m_early, 1)
        early_pc = _pieces(blocks[:lo])
        for p, e, blk in early_pc:
            sc.activation(T.ys[:, RUN * blk:RUN * (blk + e - p)], ps[:, PC - RUN * (lo - p):PC - RUN * (lo - e)], ActivationFunctionType.Copy).then_inc(S.e_early, 1)

        def quant_x(pc):
            v.wait_ge(S["ld_x%d" % pc], 16 * len(xl[pc]))
            v.quantize_mx(T.xq[:, PC * pc:PC * pc + PC], T.xp[:, PC * pc:PC * pc + PC], T.xs[:, 4 * PC * pc:4 * PC * (pc + 1)]).then_inc(S["q_x%d" % pc], 1)

        def quant_h(pc):
            oq, op = (T.aq[:], T.ap[:]) if pc == 0 else (T.fq[:, SIDE + PC * (pc - 1):SIDE + PC * pc], T.fp[:, SIDE + PC * (pc - 1):SIDE + PC * pc])
            v.wait_ge(S["a_%d" % pc], 4)
            v.quantize_mx(oq, op, T.hs[:, 4 * PC * pc:4 * PC * (pc + 1)]).then_inc(S["q_h%d" % pc], 1)

        def act_v(pc, b):
            o, i_ = views(pc, b)
            v.wait_ge(S["m%d_%d" % (pc, b)], 1)
            v.tensor_scalar(o, i_, 0.0, CONST, AluOpType.max, AluOpType.mult).then_inc(S["a_%d" % pc], 1)

        quant_x(0)
        for b in range(4):
            v.wait_ge(S["ld_w%d" % b], 16)
            v.quantize_mx(T.w1q[:, 128 * b:128 * b + 128], T.w1p[:, 128 * b:128 * b + 128], T.w1s[:, 512 * b:512 * b + 512]).then_inc(S["q_w%d" % b], 1)
        quant_x(1)
        quant_h(0)
        quant_x(2)
        act_v(1, 3)
        quant_h(1)
        act_v(2, 3)
        quant_h(2)
        v.wait_ge(S.ld_v, 16)
        v.quantize_mx(T.w2q[:], T.w2p[:], T.w2s[:]).then_inc(S.q_v, 1)
        v.wait_ge(S.m_far, 1)
        late_pc = _pieces(blocks[lo:])
        off = 7 * BANK + wl - RUN * (L - lo)
        for p, e, blk in late_pc:
            v.tensor_copy(T.ys[:, RUN * blk:RUN * (blk + e - p)], ps[:, off + RUN * p:off + RUN * e]).then_inc(S.e_late, 1)

        c0 = RUN * T.rank_of(mem[0])
        l0, l1 = min(blocks[lo:]), max(blocks[lo:]) + 1
        outside = _pieces(sorted(b for b in blocks[:lo] if not l0 <= b < l1))
        sy.wait_ge(S.e_near, 2 + len(near_pc))
        sy.dma_start(T.y[:, c0:c0 + HALF], T.ys[:, c0:c0 + HALF]).then_inc(S.st, 16)
        if outside:
            sy.wait_ge(S.e_early, len(early_pc))
        for p, e, blk in outside:
            sy.dma_start(T.y[:, RUN * blk:RUN * (blk + e - p)], T.ys[:, RUN * blk:RUN * (blk + e - p)]).then_inc(S.st, 16)
        sy.wait_ge(S.st, 16 * (1 + len(outside)))
        sc.wait_ge(S.e_early, len(early_pc))
        sc.wait_ge(S.e_late, len(late_pc))
        sc.dma_start(T.y[:, RUN * l0:RUN * l1], T.ys[:, RUN * l0:RUN * l1]).then_inc(S.st_b, 16)
        sc.wait_ge(S.st_b, 16)

        have = -1
        for call in _calls(P, topo, core):
            items = []
            for d, tag, kind, i, es in call:
                pc, sq, sp, a = _at(P, core, "n" if tag == "near" else "f", i)
                while have < pc:
                    have += 1
                    g.wait_ge(S["q_h%d" % have], 1)
                if tag == "near":
                    c, bq, bp, sem = RUN * (q if q < i else q - 1), "lq", "lp", S.near_arr
                else:
                    order, bq, bp = _slot(P, i)
                    c = RUN * order.index(q)
                    sem = S.gat_q if kind == "q" else S.gat_p
                    if tag == "dir":
                        c, bq, sem = SIDE + c, "lq", S.far_e
                if kind == "q":
                    items.append((d, T[bq][:, c:c + RUN].bitcast(u8), T[sq][:, a:a + RUN].bitcast(u8), sem, es))
                else:
                    items.append((d, T[bp][:, c:c + RUN], T[sp][:, a:a + RUN], sem, es))
            sent += _fan(g, topo, items, S.sent)

    if gate:
        for kind in "pq":
            g.wait_ge(S.gat_q if kind == "q" else S.gat_p, _due(P, topo, core, "far", kind))
            items = []
            for i, es in _cross(P, topo, core):
                _, bq, bp = _slot(P, i)
                if kind == "q":
                    lo, hi = _held(P, i)
                    items.append((far[i], T.lq[:, SIDE + RUN * lo:SIDE + RUN * hi].bitcast(u8),
                                  T[bq][:, RUN * lo:RUN * hi].bitcast(u8), S.far_l, es))
                else:
                    items.append((far[i], T.lp[:, SIDE:SIDE + HALF], T[bp][:, 0:HALF], S.far_e, es))
            sent += _fan(g, topo, items, S.sent)
    g.wait_ge(S.sent, sent)
